import numpy as np, ml_dtypes
CORES = [2,3,42,43,82,83,122,123]
N = 8
import mx_ref
BF = ml_dtypes.bfloat16
def pick(q, e):
    c = np.concatenate([q[0].reshape(128, -1, 4), np.zeros((128, 1, 4), np.uint8)], axis=1); s = np.concatenate([q[1], np.ones((16, 1), np.uint8)], axis=1)
    return (np.ascontiguousarray(c[:, e].reshape(128, -1)), np.ascontiguousarray(s[:, e]))
def join(*qs):
    return (np.concatenate([q[0] for q in qs], axis=1), np.concatenate([q[1] for q in qs], axis=1))
def put(q, e, v):
    c, s = q[0].reshape(128, -1, 4).copy(), q[1].copy(); c[:, e] = v[0].reshape(128, -1, 4); s[:, e] = v[1]
    return (c.reshape(128, -1), s)
def pk(c, s):
    return (np.ascontiguousarray(c), mx_ref.live(s))
def emit(q):
    return q[0], q[1]
def decode(q):
    o = []
    for b in range(4):
        e = np.zeros((128, 128, 4), np.float32); e[np.arange(128), np.arange(128), b] = 1
        o.append(mx_ref.matmul(mx_ref.quantize(e.reshape(128, 512).astype(BF)), q))
    return np.stack(o, axis=2).reshape(128, -1)
def cut(t, i, w=512):
    return t[:, w * i:w * i + w]
def f(rng, *shape):
    return mx_ref.flush((rng.standard_normal(shape, dtype=np.float32) * np.exp2(rng.integers(-2, 3, shape[:-1] + (1,)))).astype(BF))
def wide(rng, *shape, cols=0):
    v = rng.standard_normal(shape, dtype=np.float32) * np.exp2(rng.integers(-12, 13, shape)).astype(np.float32)
    if cols: v *= np.repeat(np.exp2(rng.integers(-cols, cols + 1, shape[:-2] + (1, shape[-1] // 4))) * (rng.random(shape[:-2] + (1, shape[-1] // 4)) > 0.0625), 4, axis=-1).astype(np.float32)
    return mx_ref.flush(v.astype(BF))
P, K, O, L = 512, 128, 1, 3
def times(t, v):
    v = t.astype(np.float32) * np.asarray(v, np.float32)
    return np.where(np.abs(v) < 2.0 ** -16, 0, v).astype(np.float32).astype(BF)
def loud(u, e):
    v = u.astype(np.float32) * np.float32(2.0 ** e)
    return np.where(np.abs(v) < 2.0 ** -30, 0, v).astype(np.float32).astype(BF)
def strong(rng, u, n):
    return np.sign(u[0, :, None, :4].astype(np.float32)) * (1 + rng.random((128, n, 4))) * 128
def near(rng, u):
    ku, v = mx_ref.quantize(np.ascontiguousarray(u[0])), np.repeat(strong(rng, u, 1), 12, axis=1).astype(np.float32)
    v[127] = 0
    z = size(ku, mx_ref.quantize(np.ascontiguousarray(v.reshape(128, -1).astype(BF))))
    v[127, 1:, 0] = np.exp2(np.floor(np.log2(z[0])) - 23 + np.arange(11))
    z = size(ku, mx_ref.quantize(np.ascontiguousarray(v.reshape(128, -1).astype(BF))))
    return v[:, [0, int(np.argmax(z > z[0]))]]
def plain(rng):
    k = np.exp2(6 * rng.random(P) - 3) * np.exp2(rng.random((N, P)) - 0.5)
    u = np.zeros((N, 128, 512), BF)
    u[:, :, :4] = f(rng, 128, 4)
    return {"gr": times(f(rng, N, 128, 4 * P), np.repeat(k, 4, axis=1)[:, None]), "u": u, "w": f(rng, N, 128, 512 * O)}
def setup_inputs(rng):
    return plain(rng)
def setup_inputs_apart(rng):
    d, h = plain(rng), K // 2
    d["u"][:, :8] = 0
    d["u"][:, 120:] = 0
    d["u"][:, 127, 0] = 1
    g = d["gr"].astype(np.float32).reshape(N, 128, P, 4) * np.float32(2.0 ** -8)
    x = rng.permutation(P)[:N // 2 * K].reshape(N // 2, 2, h)
    c = near(rng, d["u"])
    for j in range(N // 2):
        rest = rng.permutation(np.setdiff1d(np.arange(P), x[j].reshape(-1)))[:K].reshape(2, h)
        for i in range(2):
            v = c[:, (x[j, i] >= P // 2).astype(int)]
            v[:8] = (1 + rng.random((8, h, 4))) * 128 * rng.choice([-1.0, 1.0], (8, h, 4))
            g[2 * j + i][:, x[j, i]] = v * np.exp2(rng.integers(0, 3, h))[:, None]
            g[2 * j + i][:, rest[i]] = strong(rng, d["u"], h) * 2.0 ** -4
    d["gr"] = times(g.reshape(N, 128, -1), 1)
    return d
def setup_inputs_cancel(rng):
    d, m = plain(rng), K // 8
    g = d["gr"].astype(np.float32).reshape(N, 128, P, 4)
    e = rng.permutation(P)[:3 * L * m].reshape(L, 3, m)
    g[:, :, e.reshape(-1)] = 0
    for b in range(L):
        for r in range(N):
            h = (r >> b) & 1
            g[r][:, e[b, 1 + h]] = strong(rng, d["u"], m)
            if r % (1 << b) == 0:
                g[r][:, e[b, 0]] = -g[r - (1 << b)][:, e[b, 0]] if h else strong(rng, d["u"], m)
    d["gr"] = times(g.reshape(N, 128, -1), 2.0 ** -10)
    d["u"] = loud(d["u"], -26)
    return d
def setup_inputs_few(rng):
    d, m, h = plain(rng), K // 8, N // 2
    d["u"][:, :64] = 0
    g = d["gr"].astype(np.float32).reshape(N, 128, P, 4)
    g[:, 64:] = 0
    g *= (np.arange(P) % 4 != rng.integers(0, 4, (N, 1)))[:, None, :, None]
    low, e = rng.permutation(K // 4)[:m], K + rng.permutation(P - K)[:(h + 3) * m].reshape(h + 3, m)
    c = np.concatenate([low, e[0]])
    for r in range(N):
        own = e[3 + r] if r < h else e[1:3].reshape(-1)
        g[r][:, own] += strong(rng, d["u"], own.size)
        if r % 2: g[r][:, c] = -g[r - 1][:, c]
        else: g[r][:, c] += strong(rng, d["u"], c.size)
    d["gr"] = times(g.reshape(N, 128, -1), 1)
    d["u"] = loud(d["u"], 24)
    return d
def setup_inputs_spread(rng):
    d = plain(rng)
    e = rng.permutation(P)[:K]
    k = np.exp2(rng.integers(-12, -5, (N, P))) * (rng.random((N, P)) > 0.0625)
    k[:, e] = np.exp2(rng.integers(0, 7, (N, K))) * rng.choice([-1.0, 1.0], (N, K))
    g = wide(rng, N, 128, 4 * P).astype(np.float32).reshape(N, 128, P, 4)
    g[:, :, e] = np.abs(g[:, :, e]) * np.sign(d["u"][0, :, None, :4].astype(np.float32))
    d["gr"] = times(g.reshape(N, 128, -1), np.repeat(k, 4, axis=1)[:, None])
    return d
def setup_inputs_ties(rng):
    d = plain(rng)
    x = f(rng, 128, 24).astype(np.float32).reshape(128, 6, 4)
    h = np.stack([rng.permutation(P) % 6 for r in range(N)])
    sign = rng.choice([-1.0, 1.0], (N, 1, P, 1))
    d["gr"] = times((np.moveaxis(x[:, h], 1, 0) * sign).reshape(N, 128, -1), 1)
    return d
def check_inputs(d):
    b = []
    for k, lo, hi in (("gr", -16, 24), ("u", -30, 30), ("w", -30, 30)):
        v = np.abs(d[k].astype(np.float32))
        if not (np.isfinite(v).all() and ((v == 0) | (v >= 2.0 ** lo) & (v <= 2.0 ** hi)).all()): b.append("a value of " + k)
    v = d["u"].astype(np.float32)
    if (v[:, :, 4:] != 0).any(): b.append("u has numbers behind its column 0")
    if (v != v[:1]).any(): b.append("u isn't the same on all ranks")
    return b
def size(ku, q):
    return np.abs(mx_ref.matmul(ku, q)[0])
def best(s):
    return np.sort(np.argsort(-s, kind="stable")[:K])
def merge(ku, a, b):
    i, j = np.intersect1d(a[0], b[0], return_indices=True)[1:]
    q = join(a[1], b[1])
    v = decode(q).reshape(128, 2 * K, 4)
    v[:, i] = v[:, i] + v[:, K + j]
    q = put(q, i, pick(mx_ref.quantize(np.ascontiguousarray(v.reshape(128, -1).astype(BF))), i))
    n = np.concatenate([a[0], b[0]])
    e = np.setdiff1d(np.arange(2 * K), K + j)
    e = e[np.argsort(n[e])]
    e = e[best(size(ku, q)[e])]
    return n[e], pick(q, e)
def reference(gr, u, w):
    ku, S = [mx_ref.quantize(np.ascontiguousarray(u[r])) for r in range(N)], []
    for r in range(N):
        q = mx_ref.quantize(np.ascontiguousarray(gr[r]))
        e = best(size(ku[r], q))
        S.append((e, pick(q, e)))
    for b in range(L):
        new = list(S)
        for r in range(N):
            p = r ^ (1 << b)
            if r < p: new[r] = new[p] = merge(ku[r], S[r], S[p])
        S = new
    oc, osc = np.zeros((N, 128, 4 * K), np.uint8), np.zeros((N, 16, K), np.uint8)
    nb, y = np.zeros((N, 1, K), np.float32), np.zeros((N, 128, O * K), np.float32)
    for r in range(N):
        oc[r], osc[r] = emit(S[r][1])
        nb[r, 0] = S[r][0]
        for o in range(O): y[r, :, o * K:o * K + K] = mx_ref.matmul(mx_ref.quantize(np.ascontiguousarray(cut(w[r], o))), S[r][1])
    return {"oc": oc, "osc": osc, "nb": nb, "y": y}

@@ -1,0 +1,424 @@
+from concourse.mybir import dt, AluOpType as Op, AxisListType, ActivationFunctionType as Act
+
+K, P, L = 128, 512, 3
+A0, B0, M0 = 256, 384, 128
+TINY = 2.0 ** -100
+PRED = 1.0 - 2.0 ** -24
+NONE = 255.0
+SNAP = 1.5 * 2.0 ** 27
+
+SCRATCH = {}
+
+
+def _buf(name, cols, dtype, where="sbuf"):
+    SCRATCH[name] = (where, [128, cols], dtype)
+
+
+def _codes(name, cols):
+    _buf(name, cols, "float8_e4m3fn_x4")
+    _buf(name + "s", cols, "uint8")
+
+
+for _n, _c in (("ones", 512), ("ident", 128), ("tri", 128), ("tbn", 128), ("m16", 128), ("rs16", 128), ("i128", 128), ("iN", 512),
+               ("u4", 4), ("ut", 4 * 264), ("grt", 2048), ("wt", 512), ("cwt", 1536), ("et", 2560), ("dg", 512), ("ot0", 512), ("otr", 512),
+               ("tk", 512), ("nlt", 1024), ("sg0", 512), ("sg1", 512), ("c0", 512), ("c1", 512), ("rs", 1024), ("ye", 512), ("yj", 128),
+               ("xm", 128), ("sc", 128), ("xd", 128), ("xp", 128), ("xj", 128), ("posr", 128), ("mk", 128), ("um", 128), ("hm", 512),
+               ("ca", 256), ("cb", 256), ("sca", 128), ("scb", 128), ("nw0", 512), ("nw1", 512), ("nw2", 512), ("flag", 6),
+               ("ta0", 512), ("ta1", 512), ("ta2", 512)):
+    _buf(_n, _c, "bfloat16")
+for _n, _c in (("ij", 128), ("idf", 128), ("pi", 2), ("tj", 128), ("td", 128), ("tp", 4)):
+    _buf(_n, _c, "int32")
+for _n, _c in (("pf", 4), ("ar", 512), ("small", 40), ("absa", 128), ("ara", 128), ("absb", 128), ("sbm", 128), ("absm", 128),
+               ("arb", 128), ("fab", 128), ("tab", 128), ("fba", 128), ("xba", 128), ("fbb", 128), ("tbb", 128), ("nbo", 128), ("yo", 128)):
+    _buf(_n, _c, "float32")
+for _n in ("lw0", "lw1", "lw2", "lw3", "na1", "na2", "nb0", "nb1", "nb2", "off0", "off1", "off2"):
+    _buf(_n, 8, "uint16")
+for _n, _c in (("cu", 264), ("qg", 512), ("qw", 128), ("cw", 384), ("ce", 640), ("nq", 128), ("nl", 144), ("qo0", 128), ("qor", 128),
+               ("qe", 128), ("qtk", 128), ("qlt", 256), ("w0", 512), ("w1", 512), ("w2", 512), ("w3", 128), ("ap0", 128), ("ap1", 128), ("ap2", 128)):
+    _codes(_n, _c)
+SMALL = {"acol": (0, 8)}
+for _i, _n in enumerate(("aac", "sbt", "acb", "nac", "nbc", "unc", "umc", "mkc", "tka", "tkb", "tku", "tkm")):
+    SMALL[_n] = (8 + 2 * _i, 2)
+for _i in range(8):
+    _buf("p%d" % _i, 512, "float32", "psum")
+SEMAPHORES = ["sv", "sa", "st", "sp", "sent", "ac0", "ac1", "ac2", "an0", "an1", "an2"] + ["d%d" % i for i in range(16)]
+
+
+def rank_program(g, core, T, topo):
+    rank = T.rank_of(core)
+    if rank is None:
+        return
+    Q = {"v": g.vector, "a": g.scalar, "t": g.tensor, "p": g, "s": g.sync}
+    ESEM = {"v": "sv", "a": "sa", "t": "st", "p": "sp"}
+    total, known, hist, recs = {}, {e: {} for e in Q}, {}, {}
+
+    def meet(x, y):
+        if x[1] >= y[2] or y[1] >= x[2]:
+            return False
+        return not (x[3] == y[3] and x[3] > 1 and (x[1] - y[1]) % x[3])
+
+    def waits(e, outs, ins):
+        need = {}
+        for regs, isw in ((ins, False), (outs, True)):
+            for r in regs:
+                ps = SCRATCH[r[0]][0] == "psum"
+                for q, w, s, c, e2 in recs.get(r[0], []):
+                    if ps:
+                        if e2 == e and (e == "t" or not (w or isw)):
+                            continue
+                    elif not (w or isw) or not meet(r, q):
+                        continue
+                    need[s] = max(need.get(s, 0), c)
+        for s in sorted(need):
+            c = need[s]
+            if known[e].get(s, 0) < c:
+                Q[e].wait_ge(T.sem[s], c)
+                known[e][s] = c
+                for s2, c2 in hist.get((s, c), {}).items():
+                    if known[e].get(s2, 0) < c2:
+                        known[e][s2] = c2
+
+    def note(s, c, e, outs, ins):
+        for regs, w in ((ins, False), (outs, True)):
+            for r in regs:
+                recs.setdefault(r[0], []).append((r, w, s, c, e))
+
+    def op(e, call, outs, ins):
+        waits(e, outs, ins)
+        s = ESEM[e]
+        total[s] = total.get(s, 0) + 1
+        call(Q[e]).then_inc(T.sem[s], 1)
+        hist[(s, total[s])] = dict(known[e])
+        hist[(s, total[s])][s] = total[s]
+        note(s, total[s], e, outs, ins)
+
+    nd = [0]
+
+    def dma(e, out, in_, outs, ins):
+        waits(e, outs, ins)
+        s = "d%d" % nd[0]
+        nd[0] += 1
+        total[s] = 16
+        Q[e].dma_start(out, in_).then_inc(T.sem[s], 16)
+        hist[(s, 16)] = dict(known[e])
+        note(s, 16, "dma", outs, ins)
+
+    def R(n, a=0, b=None, st=1):
+        if n in SMALL:
+            o, width = SMALL[n]
+            return ("small", o + a, o + (width if b is None else b), st)
+        return (n, a, SCRATCH[n][1][1] if b is None else b, st)
+
+    def ap(r):
+        if r[3] == 1:
+            return T[r[0]][:, r[1]:r[2]]
+        return T[r[0]][:, r[1]:r[2]:r[3]]
+
+    def S(r):
+        return (r[0] + "s",) + r[1:]
+
+    def isr(x):
+        return isinstance(x, tuple)
+
+    def sap(x):
+        return ap(x) if isr(x) else x
+
+    def fill(r, c):
+        op("v", lambda q: q.memset(ap(r), c), [r], [])
+
+    def copy(o, i, e="v"):
+        if e == "v":
+            op("v", lambda q: q.tensor_copy(ap(o), ap(i)), [o], [i])
+        else:
+            op("a", lambda q: q.activation(ap(o), ap(i), Act.Copy), [o], [i])
+
+    def act(o, i, f, bias=0.0, scale=1.0, acc=None):
+        ins = [i] + [x for x in (bias, scale) if isr(x)]
+        if acc is None:
+            op("a", lambda q: q.activation(ap(o), ap(i), f, bias=sap(bias), scale=sap(scale)), [o], ins)
+        else:
+            op("a", lambda q: q.activation(ap(o), ap(i), f, accum_out=ap(acc)), [o, acc], ins)
+
+    def tt(o, a, b, f):
+        op("v", lambda q: q.tensor_tensor(ap(o), ap(a), ap(b), f), [o], [a, b])
+
+    def ts(o, i, s1, f1, s2=None, f2=None):
+        ins = [i] + [x for x in (s1, s2) if isr(x)]
+        if f2 is None:
+            op("v", lambda q: q.tensor_scalar(ap(o), ap(i), sap(s1), None, f1), [o], ins)
+        else:
+            op("v", lambda q: q.tensor_scalar(ap(o), ap(i), sap(s1), sap(s2), f1, f2), [o], ins)
+
+    def scan(o, a, b, f0, f1):
+        op("v", lambda q: q.tensor_tensor_scan(ap(o), ap(a), ap(b), 0.0, f0, f1), [o], [a, b])
+
+    def iota(o, pat, base, cm, flag=False):
+        if flag:
+            op("p", lambda q: q.iota(ap(o), pat, base, cm, allow_small_or_imprecise_dtypes=True), [o], [])
+        else:
+            op("p", lambda q: q.iota(ap(o), pat, base, cm), [o], [])
+
+    def aselect(o, i, n, f, base, cm):
+        op("p", lambda q: q.affine_select(ap(o), ap(i), [[-1, n]], f, 0.0, base, cm), [o], [i])
+
+    def gather(o, win, off, e="v"):
+        if e == "v":
+            op("v", lambda q: q.tensor_copy(ap(o), ap(win).indirect(ap(off))), [o], [win, off])
+        else:
+            op("a", lambda q: q.activation(ap(o), ap(win).indirect(ap(off)), Act.Copy), [o], [win, off])
+
+    def pick(o, win, off):
+        op("v", lambda q: q.tensor_copy(ap(o).bitcast(dt.uint32), ap(win).bitcast(dt.uint32).indirect(ap(off))), [o], [win, off])
+        gather(S(o), S(win), off, "a")
+
+    def quant(o, i):
+        op("v", lambda q: q.quantize_mx(ap(o), ap(S(o)), ap(i)), [o, S(o)], [i])
+
+    def mm(o, a, b, start=True, stop=True):
+        op("t", lambda q: q.matmul_mx(ap(o), ap(a), ap(S(a)), ap(b), ap(S(b)), start, stop), [o], [a, S(a), b, S(b)])
+
+    def wrap(row):
+        tt(R("xm"), row, R("m16"), Op.mult)
+        scan(R("sc"), R("rs16"), R("xm"), Op.mult, Op.add)
+    WR = R("sc", 15, 128, 16)
+
+    def engines(dst, a, b):
+        return sum(1 << e for e in topo.engines(core, dst)[a:b])
+
+    def send(dst, o, i, sem, a, b, raw=False):
+        waits("p", [], [i])
+        rid, pid, _se = topo.addr(dst)
+        x, y = (ap(o), ap(i)) if raw else (ap(o).bitcast(dt.uint8), ap(i).bitcast(dt.uint8))
+        g.remote_dma(x, y, T.sem[sem], T.sem["sent"], pid, rid, engines(dst, a, b))
+        total["sent"] = total.get("sent", 0) + (b - a)
+        total[sem] = total.get(sem, 0) + (b - a)
+
+    UB = R("cu", 0, 128)
+
+    def UZ(q):
+        return R("cu", 128 + 6 - 2 * q, 256 + 6 - 2 * q)
+
+    def E(t):
+        return R("ce", 128 * t, 128 * t + 128)
+
+    LO, HI, WU = R("cw", 0, 128), R("cw", 128, 256), R("cw", 256, 384)
+
+    def pb(i, n=128, a=0):
+        return R("p%d" % i, a, n)
+
+    dma("s", ap(R("u4")), T.u[:, 0:4], [R("u4")], [])
+    for q in range(4):
+        r = R("grt", 512 * q, 512 * q + 512)
+        dma("a" if q % 2 else "s", ap(r), T.gr[:, 512 * q:512 * q + 512], [r], [])
+    dma("s", ap(R("wt")), T.w[:, 0:512], [R("wt")], [])
+
+    o128 = R("ones", 0, 128)
+    fill(R("ones"), 1.0)
+    fill(R("ut"), 0.0)
+    iota(R("pi", 0, 1), [[1, 1]], 0, 1)
+    iota(R("idf"), [[1, 128]], 128, -1)
+    iota(R("ij"), [[1, 128]], 0, 0)
+    aselect(R("tri"), o128, 128, Op.is_gt, 0, 1)
+    iota(R("i128"), [[1, 128]], 0, 0, True)
+    aselect(R("ident"), o128, 128, Op.is_equal, 0, 1)
+    for b in range(4):
+        aselect(R("et", 512 * b, 512 * b + 512), R("ones"), 512, Op.is_equal, b, 4)
+    iota(R("iN"), [[1, 512]], -256, 0, True)
+    fill(R("dg"), 0.0)
+    fill(R("cwt", 1024, 1536), 0.0)
+    fill(R("ta0"), NONE)
+    fill(R("otr"), 0.0)
+    for t in range(4):
+        ts(R("ut", t, 512, 4), o128, R("u4", t, t + 1), Op.mult)
+    copy(R("ut", 4 * 134, 4 * 135), R("u4"))
+    quant(R("cu"), R("ut"))
+
+    for q in range(4):
+        a, b = 128 * q, 128 * q + 128
+        quant(R("qg", a, b), R("grt", 4 * a, 4 * b))
+        mm(pb(q), UB, R("qg", a, b))
+        mm(pb(4), R("qg", a, b), UZ(q), q == 0, q == 3)
+        act(R("ar", a, b), pb(q), Act.Abs, TINY)
+    act(R("acol"), pb(4, 8), Act.Abs, TINY)
+    ts(R("tbn"), R("tri"), 0.5, Op.subtract)
+    ts(R("tp", 0, 1), R("pi", 0, 1), 15, Op.bitwise_and)
+    ts(R("tp", 1, 2), R("pi", 0, 1), 112, Op.bitwise_and)
+    ts(R("td"), R("idf"), 15, Op.bitwise_and)
+    ts(R("tj"), R("ij"), 15, Op.bitwise_and)
+    copy(R("pf", 0, 2), R("tp", 0, 2))
+    ts(R("m16"), R("td"), 0.0, Op.is_equal)
+    ts(R("rs16"), R("tj"), 0.0, Op.is_gt)
+    ts(R("cwt", 0, 512), R("ones"), R("pf", 0, 1), Op.mult)
+    for t in range(4):
+        ts(R("cwt", 512 + t, 1024, 4), o128, R("pf", 1, 2), Op.mult, 128.0 * (t - 2), Op.add)
+    ts(R("cwt", 1024, 1536, 4), o128, -1.0, Op.mult)
+    ts(R("cwt", 1025, 1536, 4), o128, 2.0 ** -7, Op.mult)
+    quant(R("cw"), R("cwt"))
+    quant(R("nl", 16, 144), R("dg"))
+    for q in range(4):
+        sg, c = "sg%d" % (q % 2), "c%d" % (q % 2)
+        a, b = 128 * q, 128 * q + 128
+        act(R(sg), R("ar"), Act.Sign, R("acol", 2 * q, 2 * q + 1), -1.0)
+        if q > 0:
+            ts(R(c, 0, a), R(sg, 0, a), 0.0, Op.is_le)
+        if q < 3:
+            ts(R(c, b, 512), R(sg, b, 512), 0.0, Op.is_lt)
+        tt(R(c, a, b), R(sg, a, b), R("tbn"), Op.is_lt)
+        scan(R("rs", 256 * q, 256 * q + 256), R(c, 0, 256), R(c, 256, 512), Op.add, Op.add)
+        ts(R("ot0", q, 512, 4), R("i128"), R("rs", 256 * q + 255, 256 * q + 256), Op.is_equal)
+    quant(R("qo0"), R("ot0"))
+    mm(pb(5), LO, R("qo0"), True, False)
+    mm(pb(5), HI, R("qo0"), False, True)
+    wrap(pb(5))
+    ts(R("lw0"), WR, 256.0, Op.add)
+    pick(R("w0", A0, B0), R("qg"), R("lw0"))
+    partner = [T.cores[rank ^ (1 << b)] for b in range(L)]
+
+    def send_set(b):
+        w = "w%d" % b
+        send(partner[b], R(w, B0, 512), R(w, A0, B0), "ac%d" % b, 0, 4)
+        send(partner[b], R(w + "s", B0, 512), R(w + "s", A0, B0), "ac%d" % b, 4, 6, True)
+        note("ac%d" % b, 6, "far", [R(w, B0, 512), R(w + "s", B0, 512)], [])
+
+    send_set(0)
+    ts(R("dg", 0, 32, 4), WR, SNAP, Op.add, SNAP, Op.subtract)
+    tt(R("dg", 1, 32, 4), WR, R("dg", 0, 32, 4), Op.subtract)
+    quant(R("nq"), R("dg"))
+    send(partner[0], R("nl", 0, 16), R("nq", 0, 16), "an0", 6, 8)
+    send(partner[0], R("nls", 0, 16), R("nqs", 0, 16), "an0", 4, 6, True)
+    note("an0", 4, "far", [R("nl", 0, 16), R("nls", 0, 16)], [])
+    copy(R("nw0", A0, B0), pb(5), "a")
+    fill(R("et", 2048, 2560), 0.0)
+    copy(R("et", 2048, 2560, 4), R("ident"))
+    copy(R("et", 2049, 2560, 4), R("ident"))
+    quant(R("ce", 0, 512), R("et", 0, 2048))
+    quant(R("ce", 512, 640), R("et", 2048, 2560))
+
+    mine = ["lw0", "na1", "na2"]
+    for b in range(L):
+        w, nw, ta, nb, off, apn = ["%s%d" % (x, b) for x in ("w", "nw", "ta", "nb", "off", "ap")]
+        last = b == L - 1
+        own, far, mrg = R(w, A0, B0), R(w, B0, 512), R(w, M0, A0)
+        na = R(mine[b])
+        if b:
+            fill(R(ta), NONE)
+        op("v", lambda q: q.tensor_copy(ap(R(ta)).indirect(ap(na)), ap(R("i128"))), [R(ta)], [na, R("i128")])
+        mm(pb(4), UB, own)
+        mm(pb(5), own, UZ(0))
+        act(R("absa"), pb(4), Act.Abs, TINY)
+        act(R("aac", 0, 1), pb(5, 1), Act.Abs, TINY)
+        nar, nbr = R(nw, A0, B0), R(nw, B0, 512)
+        nac, nbc, unc, umc, mkc = [R(x, 0, 1) for x in ("nac", "nbc", "unc", "umc", "mkc")]
+        unb, umb, mkb = [R("flag", i, i + 1) for i in (0, 2, 4)]
+        tt(R("xd"), nar, R("ident"), Op.mult)
+        act(R("xj"), R("xd"), Act.Copy, acc=nac)
+        fill(R(nw, 0, 128), 0.0)
+        if b == 0:
+            fill(R("ye"), 0.0)
+            ts(R("ye", 1, 512, 4), o128, 1.0, Op.mult)
+            quant(R("qw"), R("wt"))
+        if last:
+            fill(R("tk"), 0.0)
+            fill(R("nlt"), 0.0)
+        if b == 0:
+            mm(pb(6), E(4), R("nl", 0, 128))
+            ts(R(nb), pb(6, 8), 256.0, Op.add)
+        gather(nbr, R("iN"), R(nb), "a")
+        aselect(R("xp"), nbr, 128, Op.is_equal, 0, 1)
+        gather(R("posr"), R(ta), R(nb))
+        wrap(R("posr"))
+        ts(R(off), WR, 127.0, Op.min)
+        pick(R(apn), own, R(off))
+        act(R("xj"), R("xp"), Act.Copy, acc=nbc)
+        ts(R("mk"), R("posr"), 200.0, Op.is_lt)
+        ts(R("um"), R("posr"), 200.0, Op.is_gt)
+        first, second = (far, R(apn)) if b == 0 else (R(apn), far)
+        for t in range(4):
+            mm(pb(t), E(t), first, True, False)
+        for t in range(4):
+            mm(pb(t), E(t), second, False, True)
+        mm(pb(6), UB, far)
+        mm(pb(7), far, UZ(0))
+        ts(R("fab"), nbr, nac, Op.is_ge, PRED, Op.max)
+        ts(R("ye", 0, 512, 4), nar, nbc, Op.is_equal)
+        quant(R("qe"), R("ye"))
+        mm(pb(4), WU, R("qe"))
+        mm(pb(5), R("qe"), WU)
+        ts(R("fba"), nar, nbc, Op.is_le, PRED, Op.max)
+        ts(R("fbb"), nbr, nbc, Op.is_ge, PRED, Op.max)
+        act(R("tab"), R("fab"), Act.Copy, 0.0, R("aac", 0, 1))
+        act(R("yj"), R("ye", 0, 512, 4), Act.Copy, acc=mkc)
+        act(umc, mkc, Act.Identity, 1.0, -1.0)
+        act(R("absb"), pb(6), Act.Abs, TINY)
+        act(R("sbt", 0, 1), pb(7, 1), Act.Identity, TINY, umc)
+        copy(unb, pb(5, 1), "a")
+        copy(unc, pb(5, 1), "a")
+        copy(umb, umc, "a")
+        copy(mkb, mkc, "a")
+        copy(R(nw, M0, A0), nbr, "a")
+        if last:
+            ts(R("nlt", 2, 1024, 4), R(nw, A0, 512), nac, Op.is_gt)
+            ts(R("nlt", 3, 1024, 4), R(nw, A0, 512), nbc, Op.is_gt)
+            quant(R("qlt"), R("nlt"))
+        for t in range(4):
+            tt(R("hm", t, 512, 4), pb(t), R("mk"), Op.mult)
+        quant(mrg, R("hm"))
+        tt(R("ara"), R("absa"), pb(4), Op.mult)
+        tt(R("ca", 0, 128), R("tri"), pb(4), Op.mult)
+        mm(pb(0), UB, mrg)
+        mm(pb(1), mrg, UZ(0))
+        act(R("absm"), pb(0), Act.Abs, TINY)
+        acb = R("acb", 0, 1)
+        act(acb, pb(1, 1), Act.Abs, R("sbt", 0, 1))
+        act(R("tbb"), R("fbb"), Act.Copy, 0.0, acb)
+        tt(R("xba"), R("ara"), R("fba"), Op.mult)
+        tt(R("sbm"), R("absb"), R("um"), Op.mult)
+        tt(R("arb"), R("absm"), R("sbm"), Op.max)
+        ts(R("cb", 0, 128), R("xba"), acb, Op.is_ge)
+        tt(R("ca", 128, 256), R("arb"), R("tab"), Op.is_gt)
+        tt(R("cb", 128, 256), R("arb"), R("tbb"), Op.is_gt)
+        scan(R("sca"), R("ca", 0, 128), R("ca", 128, 256), Op.add, Op.add)
+        scan(R("scb"), R("cb", 0, 128), R("cb", 128, 256), Op.add, Op.add)
+        ra, rb = R("sca", 127, 128), R("scb", 127, 128)
+        oa, ou, om = unb, umb, mkb
+        if last:
+            oa, ou, om = [R(x, 0, 1) for x in ("tka", "tku", "tkm")]
+            ts(R("tk", 2, 3), ra, 128.0, Op.is_lt, unc, Op.mult)
+            ts(R("tk", 3, 4), rb, 128.0, Op.is_lt)
+            quant(R("qtk"), R("tk"))
+            mm(pb(6), R("qlt", 0, 128), R("qtk"))
+            mm(pb(7), R("qlt", 128, 256), R("qtk"))
+            ts(oa, ra, 128.0, Op.is_lt, unc, Op.mult)
+            ts(ou, rb, 128.0, Op.is_lt, umc, Op.mult)
+            ts(om, rb, 128.0, Op.is_lt, mkc, Op.mult)
+            ra, rb = pb(6, 1), pb(7, 1)
+        ts(R("otr", 2, 512, 4), R("i128"), ra, Op.is_equal, oa, Op.mult)
+        ts(R("otr", 3, 512, 4), R("i128"), rb, Op.is_equal, ou, Op.mult)
+        ts(R("otr", 1, 512, 4), R("i128"), rb, Op.is_equal, om, Op.mult)
+        quant(R("qor"), R("otr"))
+        mm(pb(2), LO, R("qor"), True, False)
+        mm(pb(2), HI, R("qor"), False, True)
+        wrap(pb(2))
+        lw = R("lw%d" % (b + 1))
+        ts(lw, WR, 256.0, Op.add)
+        if not last:
+            n1 = "nw%d" % (b + 1)
+            pick(R("w%d" % (b + 1), A0, B0), R(w), lw)
+            send_set(b + 1)
+            gather(R(n1, A0, B0), R(nw), lw)
+            wrap(R(n1, A0, B0))
+            ts(R(mine[b + 1]), WR, 256.0, Op.add)
+            send(partner[b + 1], R("nb%d" % (b + 1)), R(mine[b + 1]), "an%d" % (b + 1), 6, 8, True)
+            note("an%d" % (b + 1), 2, "far", [R("nb%d" % (b + 1))], [])
+        else:
+            pick(R("w3"), R(w), lw)
+            dma("s", T.oc[:, 0:512], ap(R("w3")).bitcast(dt.uint8), [], [R("w3")])
+            mm(pb(1), R("qw"), R("w3"))
+            for k in range(4):
+                dma("a" if k == 0 else "s", T.osc[4 * k:4 * k + 4, 0:128], T["w3s"][32 * k:32 * k + 4, 0:128], [], [R("w3s")])
+            op("v", lambda q: q.tensor_scalar(ap(R("nbo")), ap(R(nw)).indirect(ap(lw)), 256.0, None, Op.add), [R("nbo")], [R(nw), lw])
+            copy(R("yo"), pb(1), "a")
+            dma("a", T.y[:, 0:128], ap(R("yo")), [], [R("yo")])
+            dma("s", T.nb[0:1, 0:128], T.nbo[0:1, 0:128], [], [R("nbo")])
+    for s in sorted(total):
+        g.wait_ge(T.sem[s], total[s])

@@ -3,7 +3,7 @@ from concourse.mybir import dt, AluOpType as Op, AxisListType, ActivationFunctio
 K, P, L = 128, 512, 3
 A0, B0, M0 = 256, 384, 128
 TINY = 2.0 ** -100
-PRED = 1.0 - 2.0 ** -24
+ULP = 2.0 ** -24
 NONE = 255.0
 SNAP = 1.5 * 2.0 ** 27
 
@@ -23,25 +23,25 @@ for _n, _c in (("ones", 512), ("ident", 128), ("tri", 128), ("tbn", 128), ("m16"
                ("u4", 4), ("ut", 4 * 264), ("grt", 2048), ("wt", 512), ("cwt", 1536), ("et", 2560), ("dg", 512), ("ot0", 512), ("otr", 512),
                ("tk", 512), ("nlt", 1024), ("sg0", 512), ("sg1", 512), ("c0", 512), ("c1", 512), ("rs", 1024), ("ye", 512), ("yj", 128),
                ("xm", 128), ("sc", 128), ("xd", 128), ("xp", 128), ("xj", 128), ("posr", 128), ("mk", 128), ("um", 128), ("hm", 512),
-               ("ca", 256), ("cb", 256), ("sca", 128), ("scb", 128), ("nw0", 512), ("nw1", 512), ("nw2", 512), ("flag", 6),
-               ("ta0", 512), ("ta1", 512), ("ta2", 512)):
+               ("ca", 256), ("cb", 256), ("lta", 128), ("ltb", 256), ("sca", 128), ("scb", 128), ("nw0", 512), ("nw1", 512), ("nw2", 512),
+               ("flag", 6), ("ta0", 512), ("ta1", 512), ("ta2", 512)):
     _buf(_n, _c, "bfloat16")
 for _n, _c in (("ij", 128), ("idf", 128), ("pi", 2), ("tj", 128), ("td", 128), ("tp", 4)):
     _buf(_n, _c, "int32")
-for _n, _c in (("pf", 4), ("ar", 512), ("small", 40), ("absa", 128), ("ara", 128), ("absb", 128), ("sbm", 128), ("absm", 128),
-               ("arb", 128), ("fab", 128), ("tab", 128), ("fba", 128), ("xba", 128), ("fbb", 128), ("tbb", 128), ("nbo", 128), ("yo", 128)):
+for _n, _c in (("pf", 4), ("f0", 128), ("t0", 128), ("ar", 512), ("small", 40), ("absa", 128), ("arow", 256), ("sbs", 128), ("sbm", 128),
+               ("absm", 128), ("ta", 128), ("tb", 256), ("nbo", 128), ("yw", 512), ("yo", 128)):
     _buf(_n, _c, "float32")
 for _n in ("lw0", "lw1", "lw2", "lw3", "na1", "na2", "nb0", "nb1", "nb2", "off0", "off1", "off2"):
     _buf(_n, 8, "uint16")
-for _n, _c in (("cu", 264), ("qg", 512), ("qw", 128), ("cw", 384), ("ce", 640), ("nq", 128), ("nl", 144), ("qo0", 128), ("qor", 128),
+for _n, _c in (("cu", 264), ("qg", 512), ("qw", 128), ("cw", 384), ("ce", 640), ("nq", 128), ("nl", 128), ("qo0", 128), ("qor", 128),
                ("qe", 128), ("qtk", 128), ("qlt", 256), ("w0", 512), ("w1", 512), ("w2", 512), ("w3", 128), ("ap0", 128), ("ap1", 128), ("ap2", 128)):
     _codes(_n, _c)
 SMALL = {"acol": (0, 8)}
-for _i, _n in enumerate(("aac", "sbt", "acb", "nac", "nbc", "unc", "umc", "mkc", "tka", "tkb", "tku", "tkm")):
+for _i, _n in enumerate(("aac", "ada", "sbt", "sbd", "acb", "acd", "nac", "nbc", "unc", "umc", "mkc", "tka", "tkb", "tku", "tkm")):
     SMALL[_n] = (8 + 2 * _i, 2)
 for _i in range(8):
     _buf("p%d" % _i, 512, "float32", "psum")
-SEMAPHORES = ["sv", "sa", "st", "sp", "sent", "ac0", "ac1", "ac2", "an0", "an1", "an2"] + ["d%d" % i for i in range(16)]
+SEMAPHORES = ["sv", "sa", "st", "sp", "sent", "ac0", "ac1", "ac2", "an0", "an1", "an2", "ready"] + ["d%d" % i for i in range(16)]
 
 
 def rank_program(g, core, T, topo):
@@ -182,16 +182,33 @@ def rank_program(g, core, T, topo):
         scan(R("sc"), R("rs16"), R("xm"), Op.mult, Op.add)
     WR = R("sc", 15, 128, 16)
 
-    def engines(dst, a, b):
-        return sum(1 << e for e in topo.engines(core, dst)[a:b])
+    partner = [T.cores[rank ^ (1 << b)] for b in range(L)]
 
-    def send(dst, o, i, sem, a, b, raw=False):
+    def route(b):
+        rid, pid, _se = topo.addr(partner[b])
+        e = topo.engines(core, partner[b])
+        return pid, rid, sum(1 << x for x in e), len(e)
+
+    def sent(sem, n):
+        total["sent"] = total.get("sent", 0) + n
+        total[sem] = total.get(sem, 0) + n
+
+    def send(b, o, i, sem, raw=False):
         waits("p", [], [i])
-        rid, pid, _se = topo.addr(dst)
+        pid, rid, mask, n = route(b)
         x, y = (ap(o), ap(i)) if raw else (ap(o).bitcast(dt.uint8), ap(i).bitcast(dt.uint8))
-        g.remote_dma(x, y, T.sem[sem], T.sem["sent"], pid, rid, engines(dst, a, b))
-        total["sent"] = total.get("sent", 0) + (b - a)
-        total[sem] = total.get(sem, 0) + (b - a)
+        g.remote_dma(x, y, T.sem[sem], T.sem["sent"], pid, rid, mask)
+        sent(sem, n)
+
+    def arrive(b, sem, outs):
+        note(sem, total[sem], "far", outs, [])
+
+    def send_codes(b):
+        send(b, R("w%d" % b, B0, 512), R("w%d" % b, A0, B0), "ac%d" % b)
+
+    def send_scales(b):
+        send(b, R("w%ds" % b, B0, 512), R("w%ds" % b, A0, B0), "ac%d" % b, True)
+        arrive(b, "ac%d" % b, [R("w%d" % b, B0, 512), R("w%ds" % b, B0, 512)])
 
     UB = R("cu", 0, 128)
 
@@ -214,7 +231,7 @@ def rank_program(g, core, T, topo):
 
     o128 = R("ones", 0, 128)
     fill(R("ones"), 1.0)
-    fill(R("ut"), 0.0)
+    fill(R("dg"), 0.0)
     iota(R("pi", 0, 1), [[1, 1]], 0, 1)
     iota(R("idf"), [[1, 128]], 128, -1)
     iota(R("ij"), [[1, 128]], 0, 0)
@@ -224,10 +241,25 @@ def rank_program(g, core, T, topo):
     for b in range(4):
         aselect(R("et", 512 * b, 512 * b + 512), R("ones"), 512, Op.is_equal, b, 4)
     iota(R("iN"), [[1, 512]], -256, 0, True)
-    fill(R("dg"), 0.0)
+    quant(R("nl"), R("dg"))
+    waits("p", [R("nl"), R("nls")], [])
+    pid, rid, mask, nready = route(0)
+    g.remote_sem_update(T.sem["ready"], T.sem["sent"], pid, rid, mask)
+    sent("ready", nready)
+    ts(R("tp", 0, 1), R("pi", 0, 1), 15, Op.bitwise_and)
+    ts(R("tp", 1, 2), R("pi", 0, 1), 112, Op.bitwise_and)
+    copy(R("pf", 0, 2), R("tp", 0, 2))
     fill(R("cwt", 1024, 1536), 0.0)
+    act(R("cwt", 0, 512), R("ones"), Act.Copy, 0.0, R("pf", 0, 1))
+    for t in range(4):
+        act(R("cwt", 512 + t, 1024, 4), o128, Act.Copy, 128.0 * (t - 2), R("pf", 1, 2))
+    act(R("cwt", 1024, 1536, 4), o128, Act.Copy, 0.0, -1.0)
+    act(R("cwt", 1025, 1536, 4), o128, Act.Copy, 0.0, 2.0 ** -7)
+    fill(R("ut", 512, 1056), 0.0)
+    fill(R("et", 2048, 2560), 0.0)
+    copy(R("et", 2048, 2560, 4), R("ident"), "a")
+    copy(R("et", 2049, 2560, 4), R("ident"), "a")
     fill(R("ta0"), NONE)
-    fill(R("otr"), 0.0)
     for t in range(4):
         ts(R("ut", t, 512, 4), o128, R("u4", t, t + 1), Op.mult)
     copy(R("ut", 4 * 134, 4 * 135), R("u4"))
@@ -240,58 +272,46 @@ def rank_program(g, core, T, topo):
         mm(pb(4), R("qg", a, b), UZ(q), q == 0, q == 3)
         act(R("ar", a, b), pb(q), Act.Abs, TINY)
     act(R("acol"), pb(4, 8), Act.Abs, TINY)
+    ts(R("f0"), R("tri"), -ULP, Op.mult, 1.0, Op.add)
     ts(R("tbn"), R("tri"), 0.5, Op.subtract)
-    ts(R("tp", 0, 1), R("pi", 0, 1), 15, Op.bitwise_and)
-    ts(R("tp", 1, 2), R("pi", 0, 1), 112, Op.bitwise_and)
     ts(R("td"), R("idf"), 15, Op.bitwise_and)
     ts(R("tj"), R("ij"), 15, Op.bitwise_and)
-    copy(R("pf", 0, 2), R("tp", 0, 2))
     ts(R("m16"), R("td"), 0.0, Op.is_equal)
     ts(R("rs16"), R("tj"), 0.0, Op.is_gt)
-    ts(R("cwt", 0, 512), R("ones"), R("pf", 0, 1), Op.mult)
-    for t in range(4):
-        ts(R("cwt", 512 + t, 1024, 4), o128, R("pf", 1, 2), Op.mult, 128.0 * (t - 2), Op.add)
-    ts(R("cwt", 1024, 1536, 4), o128, -1.0, Op.mult)
-    ts(R("cwt", 1025, 1536, 4), o128, 2.0 ** -7, Op.mult)
     quant(R("cw"), R("cwt"))
-    quant(R("nl", 16, 144), R("dg"))
     for q in range(4):
         sg, c = "sg%d" % (q % 2), "c%d" % (q % 2)
         a, b = 128 * q, 128 * q + 128
-        act(R(sg), R("ar"), Act.Sign, R("acol", 2 * q, 2 * q + 1), -1.0)
-        if q > 0:
+        aj = R("acol", 2 * q, 2 * q + 1)
+        if q == 0:
+            ts(R("t0"), R("f0"), aj, Op.mult)
+            ts(R(c, b, 512), R("ar", b, 512), aj, Op.is_gt)
+            tt(R(c, a, b), R("ar", a, b), R("t0"), Op.is_gt)
+        else:
+            act(R(sg), R("ar"), Act.Sign, aj, -1.0)
             ts(R(c, 0, a), R(sg, 0, a), 0.0, Op.is_le)
-        if q < 3:
-            ts(R(c, b, 512), R(sg, b, 512), 0.0, Op.is_lt)
-        tt(R(c, a, b), R(sg, a, b), R("tbn"), Op.is_lt)
+            if q < 3:
+                ts(R(c, b, 512), R(sg, b, 512), 0.0, Op.is_lt)
+            tt(R(c, a, b), R(sg, a, b), R("tbn"), Op.is_lt)
         scan(R("rs", 256 * q, 256 * q + 256), R(c, 0, 256), R(c, 256, 512), Op.add, Op.add)
         ts(R("ot0", q, 512, 4), R("i128"), R("rs", 256 * q + 255, 256 * q + 256), Op.is_equal)
     quant(R("qo0"), R("ot0"))
+    quant(R("ce", 0, 512), R("et", 0, 2048))
     mm(pb(5), LO, R("qo0"), True, False)
     mm(pb(5), HI, R("qo0"), False, True)
     wrap(pb(5))
     ts(R("lw0"), WR, 256.0, Op.add)
     pick(R("w0", A0, B0), R("qg"), R("lw0"))
-    partner = [T.cores[rank ^ (1 << b)] for b in range(L)]
-
-    def send_set(b):
-        w = "w%d" % b
-        send(partner[b], R(w, B0, 512), R(w, A0, B0), "ac%d" % b, 0, 4)
-        send(partner[b], R(w + "s", B0, 512), R(w + "s", A0, B0), "ac%d" % b, 4, 6, True)
-        note("ac%d" % b, 6, "far", [R(w, B0, 512), R(w + "s", B0, 512)], [])
-
-    send_set(0)
+    send_codes(0)
     ts(R("dg", 0, 32, 4), WR, SNAP, Op.add, SNAP, Op.subtract)
     tt(R("dg", 1, 32, 4), WR, R("dg", 0, 32, 4), Op.subtract)
     quant(R("nq"), R("dg"))
-    send(partner[0], R("nl", 0, 16), R("nq", 0, 16), "an0", 6, 8)
-    send(partner[0], R("nls", 0, 16), R("nqs", 0, 16), "an0", 4, 6, True)
-    note("an0", 4, "far", [R("nl", 0, 16), R("nls", 0, 16)], [])
+    g.wait_ge(T.sem["ready"], nready)
+    send(0, R("nl", 0, 16), R("nq", 0, 16), "an0")
+    send(0, R("nls", 0, 16), R("nqs", 0, 16), "an0", True)
+    arrive(0, "an0", [R("nl", 0, 16), R("nls", 0, 16)])
+    send_scales(0)
     copy(R("nw0", A0, B0), pb(5), "a")
-    fill(R("et", 2048, 2560), 0.0)
-    copy(R("et", 2048, 2560, 4), R("ident"))
-    copy(R("et", 2049, 2560, 4), R("ident"))
-    quant(R("ce", 0, 512), R("et", 0, 2048))
     quant(R("ce", 512, 640), R("et", 2048, 2560))
 
     mine = ["lw0", "na1", "na2"]
@@ -307,6 +327,7 @@ def rank_program(g, core, T, topo):
         mm(pb(5), own, UZ(0))
         act(R("absa"), pb(4), Act.Abs, TINY)
         act(R("aac", 0, 1), pb(5, 1), Act.Abs, TINY)
+        act(R("ada", 0, 1), R("aac", 0, 1), Act.Copy, 0.0, ULP)
         nar, nbr = R(nw, A0, B0), R(nw, B0, 512)
         nac, nbc, unc, umc, mkc = [R(x, 0, 1) for x in ("nac", "nbc", "unc", "umc", "mkc")]
         unb, umb, mkb = [R("flag", i, i + 1) for i in (0, 2, 4)]
@@ -316,12 +337,15 @@ def rank_program(g, core, T, topo):
         if b == 0:
             fill(R("ye"), 0.0)
             ts(R("ye", 1, 512, 4), o128, 1.0, Op.mult)
+            fill(R("otr"), 0.0)
+        if b == 1:
             quant(R("qw"), R("wt"))
         if last:
+            fill(R("yw", 0, 128), 0.0)
             fill(R("tk"), 0.0)
             fill(R("nlt"), 0.0)
         if b == 0:
-            mm(pb(6), E(4), R("nl", 0, 128))
+            mm(pb(6), E(4), R("nl"))
             ts(R(nb), pb(6, 8), 256.0, Op.add)
         gather(nbr, R("iN"), R(nb), "a")
         aselect(R("xp"), nbr, 128, Op.is_equal, 0, 1)
@@ -331,7 +355,7 @@ def rank_program(g, core, T, topo):
         pick(R(apn), own, R(off))
         act(R("xj"), R("xp"), Act.Copy, acc=nbc)
         ts(R("mk"), R("posr"), 200.0, Op.is_lt)
-        ts(R("um"), R("posr"), 200.0, Op.is_gt)
+        act(R("um"), R("mk"), Act.Identity, 1.0, -1.0)
         first, second = (far, R(apn)) if b == 0 else (R(apn), far)
         for t in range(4):
             mm(pb(t), E(t), first, True, False)
@@ -339,23 +363,19 @@ def rank_program(g, core, T, topo):
             mm(pb(t), E(t), second, False, True)
         mm(pb(6), UB, far)
         mm(pb(7), far, UZ(0))
-        ts(R("fab"), nbr, nac, Op.is_ge, PRED, Op.max)
+        ts(R("lta"), nbr, nac, Op.is_lt, -1.0, Op.mult)
         ts(R("ye", 0, 512, 4), nar, nbc, Op.is_equal)
         quant(R("qe"), R("ye"))
         mm(pb(4), WU, R("qe"))
-        mm(pb(5), R("qe"), WU)
-        ts(R("fba"), nar, nbc, Op.is_le, PRED, Op.max)
-        ts(R("fbb"), nbr, nbc, Op.is_ge, PRED, Op.max)
-        act(R("tab"), R("fab"), Act.Copy, 0.0, R("aac", 0, 1))
+        ts(R("ltb"), R(nw, A0, 512), nbc, Op.is_lt, -1.0, Op.mult)
+        act(R("ta"), R("lta"), Act.Identity, R("aac", 0, 1), R("ada", 0, 1))
         act(R("yj"), R("ye", 0, 512, 4), Act.Copy, acc=mkc)
         act(umc, mkc, Act.Identity, 1.0, -1.0)
-        act(R("absb"), pb(6), Act.Abs, TINY)
-        act(R("sbt", 0, 1), pb(7, 1), Act.Identity, TINY, umc)
-        copy(unb, pb(5, 1), "a")
-        copy(unc, pb(5, 1), "a")
         copy(umb, umc, "a")
         copy(mkb, mkc, "a")
         copy(R(nw, M0, A0), nbr, "a")
+        act(R("sbt", 0, 1), pb(7, 1), Act.Identity, TINY, umc)
+        act(R("sbd", 0, 1), R("sbt", 0, 1), Act.Copy, 0.0, ULP)
         if last:
             ts(R("nlt", 2, 1024, 4), R(nw, A0, 512), nac, Op.is_gt)
             ts(R("nlt", 3, 1024, 4), R(nw, A0, 512), nbc, Op.is_gt)
@@ -363,20 +383,27 @@ def rank_program(g, core, T, topo):
         for t in range(4):
             tt(R("hm", t, 512, 4), pb(t), R("mk"), Op.mult)
         quant(mrg, R("hm"))
-        tt(R("ara"), R("absa"), pb(4), Op.mult)
+        tt(R("sbs"), pb(6), R("um"), Op.mult)
+        act(R("sbm"), R("sbs"), Act.Abs)
+        tt(R("arow", 0, 128), R("absa"), pb(4), Op.mult)
         tt(R("ca", 0, 128), R("tri"), pb(4), Op.mult)
         mm(pb(0), UB, mrg)
         mm(pb(1), mrg, UZ(0))
+        mm(pb(5), R("qe"), WU)
+        if last:
+            mm(pb(3, 384), R("qw"), R(w, M0, 512))
+        acb, acd = R("acb", 0, 1), R("acd", 0, 1)
         act(R("absm"), pb(0), Act.Abs, TINY)
-        acb = R("acb", 0, 1)
         act(acb, pb(1, 1), Act.Abs, R("sbt", 0, 1))
-        act(R("tbb"), R("fbb"), Act.Copy, 0.0, acb)
-        tt(R("xba"), R("ara"), R("fba"), Op.mult)
-        tt(R("sbm"), R("absb"), R("um"), Op.mult)
-        tt(R("arb"), R("absm"), R("sbm"), Op.max)
-        ts(R("cb", 0, 128), R("xba"), acb, Op.is_ge)
-        tt(R("ca", 128, 256), R("arb"), R("tab"), Op.is_gt)
-        tt(R("cb", 128, 256), R("arb"), R("tbb"), Op.is_gt)
+        act(acd, pb(1, 1), Act.Abs, R("sbd", 0, 1), ULP)
+        act(R("tb"), R("ltb"), Act.Identity, acb, acd)
+        copy(unb, pb(5, 1), "a")
+        copy(unc, pb(5, 1), "a")
+        if last:
+            copy(R("yw", M0, 512), pb(3, 384), "a")
+        tt(R("arow", 128, 256), R("absm"), R("sbm"), Op.max)
+        tt(R("ca", 128, 256), R("arow", 128, 256), R("ta"), Op.is_gt)
+        tt(R("cb"), R("arow"), R("tb"), Op.is_gt)
         scan(R("sca"), R("ca", 0, 128), R("ca", 128, 256), Op.add, Op.add)
         scan(R("scb"), R("cb", 0, 128), R("cb", 128, 256), Op.add, Op.add)
         ra, rb = R("sca", 127, 128), R("scb", 127, 128)
@@ -403,22 +430,22 @@ def rank_program(g, core, T, topo):
         ts(lw, WR, 256.0, Op.add)
         if not last:
             n1 = "nw%d" % (b + 1)
+            gather(R(n1, A0, B0), R(nw), lw, "a")
             pick(R("w%d" % (b + 1), A0, B0), R(w), lw)
-            send_set(b + 1)
-            gather(R(n1, A0, B0), R(nw), lw)
             wrap(R(n1, A0, B0))
             ts(R(mine[b + 1]), WR, 256.0, Op.add)
-            send(partner[b + 1], R("nb%d" % (b + 1)), R(mine[b + 1]), "an%d" % (b + 1), 6, 8, True)
-            note("an%d" % (b + 1), 2, "far", [R("nb%d" % (b + 1))], [])
+            send_codes(b + 1)
+            send(b + 1, R("nb%d" % (b + 1)), R(mine[b + 1]), "an%d" % (b + 1), True)
+            arrive(b + 1, "an%d" % (b + 1), [R("nb%d" % (b + 1))])
+            send_scales(b + 1)
         else:
             pick(R("w3"), R(w), lw)
             dma("s", T.oc[:, 0:512], ap(R("w3")).bitcast(dt.uint8), [], [R("w3")])
-            mm(pb(1), R("qw"), R("w3"))
-            for k in range(4):
-                dma("a" if k == 0 else "s", T.osc[4 * k:4 * k + 4, 0:128], T["w3s"][32 * k:32 * k + 4, 0:128], [], [R("w3s")])
-            op("v", lambda q: q.tensor_scalar(ap(R("nbo")), ap(R(nw)).indirect(ap(lw)), 256.0, None, Op.add), [R("nbo")], [R(nw), lw])
-            copy(R("yo"), pb(1), "a")
+            gather(R("yo"), R("yw"), lw, "a")
             dma("a", T.y[:, 0:128], ap(R("yo")), [], [R("yo")])
+            for k in range(4):
+                dma("a" if k % 2 else "s", T.osc[4 * k:4 * k + 4, 0:128], T["w3s"][32 * k:32 * k + 4, 0:128], [], [R("w3s")])
+            op("v", lambda q: q.tensor_scalar(ap(R("nbo")), ap(R(nw)).indirect(ap(lw)), 256.0, None, Op.add), [R("nbo")], [R(nw), lw])
             dma("s", T.nb[0:1, 0:128], T.nbo[0:1, 0:128], [], [R("nbo")])
     for s in sorted(total):
         g.wait_ge(T.sem[s], total[s])

from concourse.mybir import dt, AluOpType as Op, AxisListType, ActivationFunctionType as Act

K, P, L = 128, 512, 3
A0, B0, M0 = 256, 384, 128
TINY = 2.0 ** -100
ULP = 2.0 ** -24
NONE = 255.0
SNAP = 1.5 * 2.0 ** 27

SCRATCH = {}


def _buf(name, cols, dtype, where="sbuf"):
    SCRATCH[name] = (where, [128, cols], dtype)


def _codes(name, cols):
    _buf(name, cols, "float8_e4m3fn_x4")
    _buf(name + "s", cols, "uint8")


for _n, _c in (("ones", 512), ("ident", 128), ("tri", 128), ("tbn", 128), ("m16", 128), ("rs16", 128), ("i128", 128), ("iN", 512),
               ("u4", 4), ("ut", 4 * 264), ("grt", 2048), ("wt", 512), ("cwt", 1536), ("et", 2560), ("dg", 512), ("ot0", 512), ("otr", 512),
               ("tk", 512), ("nlt", 1024), ("sg0", 512), ("sg1", 512), ("c0", 512), ("c1", 512), ("rs", 1024), ("ye", 512), ("yj", 128),
               ("xm", 128), ("sc", 128), ("xd", 128), ("xp", 128), ("xj", 128), ("posr", 128), ("mk", 128), ("um", 128), ("hm", 512),
               ("ca", 256), ("cb", 256), ("lta", 128), ("ltb", 256), ("sca", 128), ("scb", 128), ("nw0", 512), ("nw1", 512), ("nw2", 512),
               ("flag", 6), ("ta0", 512), ("ta1", 512), ("ta2", 512)):
    _buf(_n, _c, "bfloat16")
for _n, _c in (("ij", 128), ("idf", 128), ("pi", 2), ("tj", 128), ("td", 128), ("tp", 4)):
    _buf(_n, _c, "int32")
for _n, _c in (("pf", 4), ("f0", 128), ("t0", 128), ("ar", 512), ("small", 40), ("absa", 128), ("arow", 256), ("sbs", 128), ("sbm", 128),
               ("absm", 128), ("ta", 128), ("tb", 256), ("nbo", 128), ("yw", 512), ("yo", 128)):
    _buf(_n, _c, "float32")
for _n in ("lw0", "lw1", "lw2", "lw3", "na1", "na2", "nb0", "nb1", "nb2", "off0", "off1", "off2"):
    _buf(_n, 8, "uint16")
for _n, _c in (("cu", 264), ("qg", 512), ("qw", 128), ("cw", 384), ("ce", 640), ("nq", 128), ("nl", 128), ("qo0", 128), ("qor", 128),
               ("qe", 128), ("qtk", 128), ("qlt", 256), ("w0", 512), ("w1", 512), ("w2", 512), ("w3", 128), ("ap0", 128), ("ap1", 128), ("ap2", 128)):
    _codes(_n, _c)
SMALL = {"acol": (0, 8)}
for _i, _n in enumerate(("aac", "ada", "sbt", "sbd", "acb", "acd", "nac", "nbc", "unc", "umc", "mkc", "tka", "tkb", "tku", "tkm")):
    SMALL[_n] = (8 + 2 * _i, 2)
for _i in range(8):
    _buf("p%d" % _i, 512, "float32", "psum")
SEMAPHORES = ["sv", "sa", "st", "sp", "sent", "ac0", "ac1", "ac2", "an0", "an1", "an2", "ready"] + ["d%d" % i for i in range(16)]


def rank_program(g, core, T, topo):
    rank = T.rank_of(core)
    if rank is None:
        return
    Q = {"v": g.vector, "a": g.scalar, "t": g.tensor, "p": g, "s": g.sync}
    ESEM = {"v": "sv", "a": "sa", "t": "st", "p": "sp"}
    total, known, hist, recs = {}, {e: {} for e in Q}, {}, {}

    def meet(x, y):
        if x[1] >= y[2] or y[1] >= x[2]:
            return False
        return not (x[3] == y[3] and x[3] > 1 and (x[1] - y[1]) % x[3])

    def waits(e, outs, ins):
        need = {}
        for regs, isw in ((ins, False), (outs, True)):
            for r in regs:
                ps = SCRATCH[r[0]][0] == "psum"
                for q, w, s, c, e2 in recs.get(r[0], []):
                    if ps:
                        if e2 == e and (e == "t" or not (w or isw)):
                            continue
                    elif not (w or isw) or not meet(r, q):
                        continue
                    need[s] = max(need.get(s, 0), c)
        for s in sorted(need):
            c = need[s]
            if known[e].get(s, 0) < c:
                Q[e].wait_ge(T.sem[s], c)
                known[e][s] = c
                for s2, c2 in hist.get((s, c), {}).items():
                    if known[e].get(s2, 0) < c2:
                        known[e][s2] = c2

    def note(s, c, e, outs, ins):
        for regs, w in ((ins, False), (outs, True)):
            for r in regs:
                recs.setdefault(r[0], []).append((r, w, s, c, e))

    def op(e, call, outs, ins):
        waits(e, outs, ins)
        s = ESEM[e]
        total[s] = total.get(s, 0) + 1
        call(Q[e]).then_inc(T.sem[s], 1)
        hist[(s, total[s])] = dict(known[e])
        hist[(s, total[s])][s] = total[s]
        note(s, total[s], e, outs, ins)

    nd = [0]

    def dma(e, out, in_, outs, ins):
        waits(e, outs, ins)
        s = "d%d" % nd[0]
        nd[0] += 1
        total[s] = 16
        Q[e].dma_start(out, in_).then_inc(T.sem[s], 16)
        hist[(s, 16)] = dict(known[e])
        note(s, 16, "dma", outs, ins)

    def R(n, a=0, b=None, st=1):
        if n in SMALL:
            o, width = SMALL[n]
            return ("small", o + a, o + (width if b is None else b), st)
        return (n, a, SCRATCH[n][1][1] if b is None else b, st)

    def ap(r):
        if r[3] == 1:
            return T[r[0]][:, r[1]:r[2]]
        return T[r[0]][:, r[1]:r[2]:r[3]]

    def S(r):
        return (r[0] + "s",) + r[1:]

    def isr(x):
        return isinstance(x, tuple)

    def sap(x):
        return ap(x) if isr(x) else x

    def fill(r, c):
        op("v", lambda q: q.memset(ap(r), c), [r], [])

    def copy(o, i, e="v"):
        if e == "v":
            op("v", lambda q: q.tensor_copy(ap(o), ap(i)), [o], [i])
        else:
            op("a", lambda q: q.activation(ap(o), ap(i), Act.Copy), [o], [i])

    def act(o, i, f, bias=0.0, scale=1.0, acc=None):
        ins = [i] + [x for x in (bias, scale) if isr(x)]
        if acc is None:
            op("a", lambda q: q.activation(ap(o), ap(i), f, bias=sap(bias), scale=sap(scale)), [o], ins)
        else:
            op("a", lambda q: q.activation(ap(o), ap(i), f, accum_out=ap(acc)), [o, acc], ins)

    def tt(o, a, b, f):
        op("v", lambda q: q.tensor_tensor(ap(o), ap(a), ap(b), f), [o], [a, b])

    def ts(o, i, s1, f1, s2=None, f2=None):
        ins = [i] + [x for x in (s1, s2) if isr(x)]
        if f2 is None:
            op("v", lambda q: q.tensor_scalar(ap(o), ap(i), sap(s1), None, f1), [o], ins)
        else:
            op("v", lambda q: q.tensor_scalar(ap(o), ap(i), sap(s1), sap(s2), f1, f2), [o], ins)

    def scan(o, a, b, f0, f1):
        op("v", lambda q: q.tensor_tensor_scan(ap(o), ap(a), ap(b), 0.0, f0, f1), [o], [a, b])

    def iota(o, pat, base, cm, flag=False):
        if flag:
            op("p", lambda q: q.iota(ap(o), pat, base, cm, allow_small_or_imprecise_dtypes=True), [o], [])
        else:
            op("p", lambda q: q.iota(ap(o), pat, base, cm), [o], [])

    def aselect(o, i, n, f, base, cm):
        op("p", lambda q: q.affine_select(ap(o), ap(i), [[-1, n]], f, 0.0, base, cm), [o], [i])

    def gather(o, win, off, e="v"):
        if e == "v":
            op("v", lambda q: q.tensor_copy(ap(o), ap(win).indirect(ap(off))), [o], [win, off])
        else:
            op("a", lambda q: q.activation(ap(o), ap(win).indirect(ap(off)), Act.Copy), [o], [win, off])

    def pick(o, win, off):
        op("v", lambda q: q.tensor_copy(ap(o).bitcast(dt.uint32), ap(win).bitcast(dt.uint32).indirect(ap(off))), [o], [win, off])
        gather(S(o), S(win), off, "a")

    def quant(o, i):
        op("v", lambda q: q.quantize_mx(ap(o), ap(S(o)), ap(i)), [o, S(o)], [i])

    def mm(o, a, b, start=True, stop=True):
        op("t", lambda q: q.matmul_mx(ap(o), ap(a), ap(S(a)), ap(b), ap(S(b)), start, stop), [o], [a, S(a), b, S(b)])

    def wrap(row):
        tt(R("xm"), row, R("m16"), Op.mult)
        scan(R("sc"), R("rs16"), R("xm"), Op.mult, Op.add)
    WR = R("sc", 15, 128, 16)

    partner = [T.cores[rank ^ (1 << b)] for b in range(L)]

    def route(b):
        rid, pid, _se = topo.addr(partner[b])
        e = topo.engines(core, partner[b])
        return pid, rid, sum(1 << x for x in e), len(e)

    def sent(sem, n):
        total["sent"] = total.get("sent", 0) + n
        total[sem] = total.get(sem, 0) + n

    def send(b, o, i, sem, raw=False):
        waits("p", [], [i])
        pid, rid, mask, n = route(b)
        x, y = (ap(o), ap(i)) if raw else (ap(o).bitcast(dt.uint8), ap(i).bitcast(dt.uint8))
        g.remote_dma(x, y, T.sem[sem], T.sem["sent"], pid, rid, mask)
        sent(sem, n)

    def arrive(b, sem, outs):
        note(sem, total[sem], "far", outs, [])

    def send_codes(b):
        send(b, R("w%d" % b, B0, 512), R("w%d" % b, A0, B0), "ac%d" % b)

    def send_scales(b):
        send(b, R("w%ds" % b, B0, 512), R("w%ds" % b, A0, B0), "ac%d" % b, True)
        arrive(b, "ac%d" % b, [R("w%d" % b, B0, 512), R("w%ds" % b, B0, 512)])

    UB = R("cu", 0, 128)

    def UZ(q):
        return R("cu", 128 + 6 - 2 * q, 256 + 6 - 2 * q)

    def E(t):
        return R("ce", 128 * t, 128 * t + 128)

    LO, HI, WU = R("cw", 0, 128), R("cw", 128, 256), R("cw", 256, 384)

    def pb(i, n=128, a=0):
        return R("p%d" % i, a, n)

    dma("s", ap(R("u4")), T.u[:, 0:4], [R("u4")], [])
    for q in range(4):
        r = R("grt", 512 * q, 512 * q + 512)
        dma("a" if q % 2 else "s", ap(r), T.gr[:, 512 * q:512 * q + 512], [r], [])
    dma("s", ap(R("wt")), T.w[:, 0:512], [R("wt")], [])

    o128 = R("ones", 0, 128)
    fill(R("ones"), 1.0)
    fill(R("dg"), 0.0)
    iota(R("pi", 0, 1), [[1, 1]], 0, 1)
    iota(R("idf"), [[1, 128]], 128, -1)
    iota(R("ij"), [[1, 128]], 0, 0)
    aselect(R("tri"), o128, 128, Op.is_gt, 0, 1)
    iota(R("i128"), [[1, 128]], 0, 0, True)
    aselect(R("ident"), o128, 128, Op.is_equal, 0, 1)
    for b in range(4):
        aselect(R("et", 512 * b, 512 * b + 512), R("ones"), 512, Op.is_equal, b, 4)
    iota(R("iN"), [[1, 512]], -256, 0, True)
    quant(R("nl"), R("dg"))
    waits("p", [R("nl"), R("nls")], [])
    pid, rid, mask, nready = route(0)
    g.remote_sem_update(T.sem["ready"], T.sem["sent"], pid, rid, mask)
    sent("ready", nready)
    ts(R("tp", 0, 1), R("pi", 0, 1), 15, Op.bitwise_and)
    ts(R("tp", 1, 2), R("pi", 0, 1), 112, Op.bitwise_and)
    copy(R("pf", 0, 2), R("tp", 0, 2))
    fill(R("cwt", 1024, 1536), 0.0)
    act(R("cwt", 0, 512), R("ones"), Act.Copy, 0.0, R("pf", 0, 1))
    for t in range(4):
        act(R("cwt", 512 + t, 1024, 4), o128, Act.Copy, 128.0 * (t - 2), R("pf", 1, 2))
    act(R("cwt", 1024, 1536, 4), o128, Act.Copy, 0.0, -1.0)
    act(R("cwt", 1025, 1536, 4), o128, Act.Copy, 0.0, 2.0 ** -7)
    fill(R("ut", 512, 1056), 0.0)
    fill(R("et", 2048, 2560), 0.0)
    copy(R("et", 2048, 2560, 4), R("ident"), "a")
    copy(R("et", 2049, 2560, 4), R("ident"), "a")
    fill(R("ta0"), NONE)
    for t in range(4):
        ts(R("ut", t, 512, 4), o128, R("u4", t, t + 1), Op.mult)
    copy(R("ut", 4 * 134, 4 * 135), R("u4"))
    quant(R("cu"), R("ut"))

    for q in range(4):
        a, b = 128 * q, 128 * q + 128
        quant(R("qg", a, b), R("grt", 4 * a, 4 * b))
        mm(pb(q), UB, R("qg", a, b))
        mm(pb(4), R("qg", a, b), UZ(q), q == 0, q == 3)
        act(R("ar", a, b), pb(q), Act.Abs, TINY)
    act(R("acol"), pb(4, 8), Act.Abs, TINY)
    ts(R("f0"), R("tri"), -ULP, Op.mult, 1.0, Op.add)
    ts(R("tbn"), R("tri"), 0.5, Op.subtract)
    ts(R("td"), R("idf"), 15, Op.bitwise_and)
    ts(R("tj"), R("ij"), 15, Op.bitwise_and)
    ts(R("m16"), R("td"), 0.0, Op.is_equal)
    ts(R("rs16"), R("tj"), 0.0, Op.is_gt)
    quant(R("cw"), R("cwt"))
    for q in range(4):
        sg, c = "sg%d" % (q % 2), "c%d" % (q % 2)
        a, b = 128 * q, 128 * q + 128
        aj = R("acol", 2 * q, 2 * q + 1)
        if q == 0:
            ts(R("t0"), R("f0"), aj, Op.mult)
            ts(R(c, b, 512), R("ar", b, 512), aj, Op.is_gt)
            tt(R(c, a, b), R("ar", a, b), R("t0"), Op.is_gt)
        else:
            act(R(sg), R("ar"), Act.Sign, aj, -1.0)
            ts(R(c, 0, a), R(sg, 0, a), 0.0, Op.is_le)
            if q < 3:
                ts(R(c, b, 512), R(sg, b, 512), 0.0, Op.is_lt)
            tt(R(c, a, b), R(sg, a, b), R("tbn"), Op.is_lt)
        scan(R("rs", 256 * q, 256 * q + 256), R(c, 0, 256), R(c, 256, 512), Op.add, Op.add)
        ts(R("ot0", q, 512, 4), R("i128"), R("rs", 256 * q + 255, 256 * q + 256), Op.is_equal)
    quant(R("qo0"), R("ot0"))
    quant(R("ce", 0, 512), R("et", 0, 2048))
    mm(pb(5), LO, R("qo0"), True, False)
    mm(pb(5), HI, R("qo0"), False, True)
    wrap(pb(5))
    ts(R("lw0"), WR, 256.0, Op.add)
    pick(R("w0", A0, B0), R("qg"), R("lw0"))
    send_codes(0)
    ts(R("dg", 0, 32, 4), WR, SNAP, Op.add, SNAP, Op.subtract)
    tt(R("dg", 1, 32, 4), WR, R("dg", 0, 32, 4), Op.subtract)
    quant(R("nq"), R("dg"))
    g.wait_ge(T.sem["ready"], nready)
    send(0, R("nl", 0, 16), R("nq", 0, 16), "an0")
    send(0, R("nls", 0, 16), R("nqs", 0, 16), "an0", True)
    arrive(0, "an0", [R("nl", 0, 16), R("nls", 0, 16)])
    send_scales(0)
    copy(R("nw0", A0, B0), pb(5), "a")
    quant(R("ce", 512, 640), R("et", 2048, 2560))

    mine = ["lw0", "na1", "na2"]
    for b in range(L):
        w, nw, ta, nb, off, apn = ["%s%d" % (x, b) for x in ("w", "nw", "ta", "nb", "off", "ap")]
        last = b == L - 1
        own, far, mrg = R(w, A0, B0), R(w, B0, 512), R(w, M0, A0)
        na = R(mine[b])
        if b:
            fill(R(ta), NONE)
        op("v", lambda q: q.tensor_copy(ap(R(ta)).indirect(ap(na)), ap(R("i128"))), [R(ta)], [na, R("i128")])
        mm(pb(4), UB, own)
        mm(pb(5), own, UZ(0))
        act(R("absa"), pb(4), Act.Abs, TINY)
        act(R("aac", 0, 1), pb(5, 1), Act.Abs, TINY)
        act(R("ada", 0, 1), R("aac", 0, 1), Act.Copy, 0.0, ULP)
        nar, nbr = R(nw, A0, B0), R(nw, B0, 512)
        nac, nbc, unc, umc, mkc = [R(x, 0, 1) for x in ("nac", "nbc", "unc", "umc", "mkc")]
        unb, umb, mkb = [R("flag", i, i + 1) for i in (0, 2, 4)]
        tt(R("xd"), nar, R("ident"), Op.mult)
        act(R("xj"), R("xd"), Act.Copy, acc=nac)
        fill(R(nw, 0, 128), 0.0)
        if b == 0:
            fill(R("ye"), 0.0)
            ts(R("ye", 1, 512, 4), o128, 1.0, Op.mult)
            fill(R("otr"), 0.0)
        if b == 1:
            quant(R("qw"), R("wt"))
        if last:
            fill(R("yw", 0, 128), 0.0)
            fill(R("tk"), 0.0)
            fill(R("nlt"), 0.0)
        if b == 0:
            mm(pb(6), E(4), R("nl"))
            ts(R(nb), pb(6, 8), 256.0, Op.add)
        gather(nbr, R("iN"), R(nb), "a")
        aselect(R("xp"), nbr, 128, Op.is_equal, 0, 1)
        gather(R("posr"), R(ta), R(nb))
        wrap(R("posr"))
        ts(R(off), WR, 127.0, Op.min)
        pick(R(apn), own, R(off))
        act(R("xj"), R("xp"), Act.Copy, acc=nbc)
        ts(R("mk"), R("posr"), 200.0, Op.is_lt)
        act(R("um"), R("mk"), Act.Identity, 1.0, -1.0)
        first, second = (far, R(apn)) if b == 0 else (R(apn), far)
        for t in range(4):
            mm(pb(t), E(t), first, True, False)
        for t in range(4):
            mm(pb(t), E(t), second, False, True)
        mm(pb(6), UB, far)
        mm(pb(7), far, UZ(0))
        ts(R("lta"), nbr, nac, Op.is_lt, -1.0, Op.mult)
        ts(R("ye", 0, 512, 4), nar, nbc, Op.is_equal)
        quant(R("qe"), R("ye"))
        mm(pb(4), WU, R("qe"))
        ts(R("ltb"), R(nw, A0, 512), nbc, Op.is_lt, -1.0, Op.mult)
        act(R("ta"), R("lta"), Act.Identity, R("aac", 0, 1), R("ada", 0, 1))
        act(R("yj"), R("ye", 0, 512, 4), Act.Copy, acc=mkc)
        act(umc, mkc, Act.Identity, 1.0, -1.0)
        copy(umb, umc, "a")
        copy(mkb, mkc, "a")
        copy(R(nw, M0, A0), nbr, "a")
        act(R("sbt", 0, 1), pb(7, 1), Act.Identity, TINY, umc)
        act(R("sbd", 0, 1), R("sbt", 0, 1), Act.Copy, 0.0, ULP)
        if last:
            ts(R("nlt", 2, 1024, 4), R(nw, A0, 512), nac, Op.is_gt)
            ts(R("nlt", 3, 1024, 4), R(nw, A0, 512), nbc, Op.is_gt)
            quant(R("qlt"), R("nlt"))
        for t in range(4):
            tt(R("hm", t, 512, 4), pb(t), R("mk"), Op.mult)
        quant(mrg, R("hm"))
        tt(R("sbs"), pb(6), R("um"), Op.mult)
        act(R("sbm"), R("sbs"), Act.Abs)
        tt(R("arow", 0, 128), R("absa"), pb(4), Op.mult)
        tt(R("ca", 0, 128), R("tri"), pb(4), Op.mult)
        mm(pb(0), UB, mrg)
        mm(pb(1), mrg, UZ(0))
        mm(pb(5), R("qe"), WU)
        if last:
            mm(pb(3, 384), R("qw"), R(w, M0, 512))
        acb, acd = R("acb", 0, 1), R("acd", 0, 1)
        act(R("absm"), pb(0), Act.Abs, TINY)
        act(acb, pb(1, 1), Act.Abs, R("sbt", 0, 1))
        act(acd, pb(1, 1), Act.Abs, R("sbd", 0, 1), ULP)
        act(R("tb"), R("ltb"), Act.Identity, acb, acd)
        copy(unb, pb(5, 1), "a")
        copy(unc, pb(5, 1), "a")
        if last:
            copy(R("yw", M0, 512), pb(3, 384), "a")
        tt(R("arow", 128, 256), R("absm"), R("sbm"), Op.max)
        tt(R("ca", 128, 256), R("arow", 128, 256), R("ta"), Op.is_gt)
        tt(R("cb"), R("arow"), R("tb"), Op.is_gt)
        scan(R("sca"), R("ca", 0, 128), R("ca", 128, 256), Op.add, Op.add)
        scan(R("scb"), R("cb", 0, 128), R("cb", 128, 256), Op.add, Op.add)
        ra, rb = R("sca", 127, 128), R("scb", 127, 128)
        oa, ou, om = unb, umb, mkb
        if last:
            oa, ou, om = [R(x, 0, 1) for x in ("tka", "tku", "tkm")]
            ts(R("tk", 2, 3), ra, 128.0, Op.is_lt, unc, Op.mult)
            ts(R("tk", 3, 4), rb, 128.0, Op.is_lt)
            quant(R("qtk"), R("tk"))
            mm(pb(6), R("qlt", 0, 128), R("qtk"))
            mm(pb(7), R("qlt", 128, 256), R("qtk"))
            ts(oa, ra, 128.0, Op.is_lt, unc, Op.mult)
            ts(ou, rb, 128.0, Op.is_lt, umc, Op.mult)
            ts(om, rb, 128.0, Op.is_lt, mkc, Op.mult)
            ra, rb = pb(6, 1), pb(7, 1)
        ts(R("otr", 2, 512, 4), R("i128"), ra, Op.is_equal, oa, Op.mult)
        ts(R("otr", 3, 512, 4), R("i128"), rb, Op.is_equal, ou, Op.mult)
        ts(R("otr", 1, 512, 4), R("i128"), rb, Op.is_equal, om, Op.mult)
        quant(R("qor"), R("otr"))
        mm(pb(2), LO, R("qor"), True, False)
        mm(pb(2), HI, R("qor"), False, True)
        wrap(pb(2))
        lw = R("lw%d" % (b + 1))
        ts(lw, WR, 256.0, Op.add)
        if not last:
            n1 = "nw%d" % (b + 1)
            gather(R(n1, A0, B0), R(nw), lw, "a")
            pick(R("w%d" % (b + 1), A0, B0), R(w), lw)
            wrap(R(n1, A0, B0))
            ts(R(mine[b + 1]), WR, 256.0, Op.add)
            send_codes(b + 1)
            send(b + 1, R("nb%d" % (b + 1)), R(mine[b + 1]), "an%d" % (b + 1), True)
            arrive(b + 1, "an%d" % (b + 1), [R("nb%d" % (b + 1))])
            send_scales(b + 1)
        else:
            pick(R("w3"), R(w), lw)
            dma("s", T.oc[:, 0:512], ap(R("w3")).bitcast(dt.uint8), [], [R("w3")])
            gather(R("yo"), R("yw"), lw, "a")
            dma("a", T.y[:, 0:128], ap(R("yo")), [], [R("yo")])
            for k in range(4):
                dma("a" if k % 2 else "s", T.osc[4 * k:4 * k + 4, 0:128], T["w3s"][32 * k:32 * k + 4, 0:128], [], [R("w3s")])
            op("v", lambda q: q.tensor_scalar(ap(R("nbo")), ap(R(nw)).indirect(ap(lw)), 256.0, None, Op.add), [R("nbo")], [R(nw), lw])
            dma("s", T.nb[0:1, 0:128], T.nbo[0:1, 0:128], [], [R("nbo")])
    for s in sorted(total):
        g.wait_ge(T.sem[s], total[s])
